import numpy as np
import ml_dtypes


def mxq(x, axis, fmt="e4m3"):
    dtype, down = {"e4m3": (ml_dtypes.float8_e4m3fn, 7), "e5m2": (ml_dtypes.float8_e5m2, 14)}[fmt]
    v = np.moveaxis(np.asarray(x, np.float32).astype(ml_dtypes.bfloat16).astype(np.float64), axis, -1)
    blocks = v.reshape(v.shape[:-1] + (-1, 32))
    amax = np.abs(blocks).max(-1, keepdims=True)
    byte = np.maximum(np.where(amax > 0, np.frexp(amax)[1] - 1 + 127, 0) - down, 1)
    scale = np.exp2(byte - 127.0)
    codes = (blocks / scale).astype(np.float32).astype(dtype).astype(np.float64)
    return np.moveaxis((codes * scale).reshape(v.shape), -1, axis)


WIDE = False


def mx_kscale(k):
    if not WIDE:
        return np.ones(k)
    levels = np.array([24, -24, 12, -12, 0])
    if k % 512:
        return np.exp2(np.random.permutation(np.resize(levels, k // 32))).repeat(32)
    a = np.empty((k // 512, 16))
    for p in range(k // 512):
        a[p, :8] = np.random.permutation(np.resize(levels, 8))
        for g in range(8):
            far = levels[np.abs(levels - a[p, g]) >= 10]
            a[p, g + 8] = far[np.random.randint(len(far))]
    return np.exp2(a.ravel()).repeat(32)


def f64(x):
    return np.asarray(x).astype(np.float64)


def striped(idx):
    return np.tile(idx.reshape(-1, 16).T, (8, 1)).astype(np.uint16)


def unstriped(offs):
    return offs[:16].T.reshape(-1).astype(np.int64)


E2M1 = np.array([0.0, 0.5, 1.0, 1.5, 2.0, 3.0, 4.0, 6.0, -0.0, -0.5, -1.0, -1.5, -2.0, -3.0, -4.0, -6.0])


def pack_weight(w, fmt):
    k, n = w.shape
    w = f64(np.asarray(w, np.float32).astype(ml_dtypes.bfloat16)).reshape(k // 32, 32, n)
    amax = np.abs(w).max(1)
    if fmt == "e4m3":
        byte = np.frexp(amax)[1] - 1 + 127 - 7
    else:
        mant, ex = np.frexp(amax / 6.0)
        byte = np.where(mant > 0.5, ex, ex - 1) + 127
    byte = np.clip(np.where(amax > 0, byte, 1), 1, 254)
    scaled = (w * np.exp2(127.0 - byte)[:, None, :]).reshape(k, n).astype(np.float32)
    by_word = np.ascontiguousarray(scaled.reshape(k // 512, 128, 4, n).transpose(0, 1, 3, 2))
    if fmt == "e4m3":
        words = by_word.astype(ml_dtypes.float8_e4m3fn).view(np.uint8)
    else:
        c = by_word.astype(ml_dtypes.float4_e2m1fn).view(np.uint8) & 0xF
        words = (c[..., 0::2] | (c[..., 1::2] << 4)).reshape(k // 512, 128, 2 * n)
    return np.ascontiguousarray(words), np.ascontiguousarray(byte.astype(np.uint8).reshape(k // 512, 16, n))


def unpack_weight(words, scales, fmt):
    g, _, n = scales.shape
    words = np.ascontiguousarray(words).reshape(g, 128, n, -1)
    if fmt == "e4m3":
        vals = words.view(ml_dtypes.float8_e4m3fn).astype(np.float64)
    else:
        nib = np.empty((g, 128, n, 4), np.uint8)
        nib[..., 0::2] = words & 0xF
        nib[..., 1::2] = words >> 4
        vals = E2M1[nib]
    vals = vals * np.repeat(np.exp2(scales.astype(np.float64) - 127.0), 8, axis=1)[..., None]
    return vals.transpose(0, 1, 3, 2).reshape(g * 512, n)


K, R, M, T, N, J = 512, 1024, 1024, 4096, 256, 2048


def setup_inputs():
    n = np.random.standard_normal
    u = mx_kscale(R)[:, None]
    s = mx_kscale(K)[:, None]
    p_tab = pack_weight(n((R, T)) * u, "e4m3")
    return {
        "x": (n((K, M)) * s).astype(np.float32),
        "w": (n((K, R)) / np.sqrt(K) / s / u.T).astype(np.float32),
        "tab_words": p_tab[0],
        "tab_scales": p_tab[1],
        "wv": (n((R, N)) / np.sqrt(R) / u).astype(np.float32),
        "offs": striped(np.random.permutation(T)[:J]),
    }


def reference(x, w, tab_words, tab_scales, wv, offs):
    idx = unstriped(offs)
    x_ = mxq(f64(x), 0, "e4m3")
    w_ = mxq(f64(w), 0, "e4m3")
    qa = w_.T @ x_
    qa_ = mxq(qa, 0, "e4m3")
    tab_ = unpack_weight(tab_words, tab_scales, "e4m3")[:, idx]
    sc = qa_.T @ tab_
    wv_ = mxq(f64(wv), 0, "e4m3")
    vv = wv_.T @ tab_
    return 8.0 * np.tanh(sc * 0.00390625), vv

@@ -1,0 +1,224 @@
+from contextlib import ExitStack
+
+import concourse.mybir as mybir
+
+K, R, M, T, N, J = 512, 1024, 1024, 4096, 256, 2048
+FLOPS = 2 * K * R * M + 2 * R * M * J + 2 * R * N * J
+
+F32 = mybir.dt.float32
+BF16 = mybir.dt.bfloat16
+I32 = mybir.dt.int32
+U32 = mybir.dt.uint32
+U16 = mybir.dt.uint16
+U8 = mybir.dt.uint8
+FP8X4 = mybir.dt.float8_e4m3fn_x4
+TANH = mybir.ActivationFunctionType.Tanh
+MULT = mybir.AluOpType.mult
+
+P = 128
+PACK = 4
+PASSES = 2
+JW = 512
+NJ = J // JW
+XW = 512
+
+
+def tile_list_mlat_cap_kernel(tc, x, w, tab_words, tab_scales, wv, offs, out_0, out_1):
+    nc = tc.nc
+    with ExitStack() as ctx:
+        keep = ctx.enter_context(tc.tile_pool(name="keep", bufs=1))
+        qa_psum = ctx.enter_context(tc.psum_pool(name="qa_psum", bufs=2))
+        psum = ctx.enter_context(tc.psum_pool(name="psum", bufs=6))
+
+        def tile(shape, dtype, name):
+            return keep.tile(shape, dtype, name=name, align_bytes=64)
+
+        offsets = keep.tile([P, J // 16], U16, name="offsets")
+        w_raw = [tile([P, PACK, 512], F32, "w_raw%d" % a) for a in range(PASSES)]
+        x_raw = [tile([P, PACK, XW], F32, "x_raw%d" % h) for h in range(M // XW)]
+        wv_raw = tile([P, PASSES, PACK, N], F32, "wv_raw")
+        words = [tile([P, T], I32, "words%d" % a) for a in range(PASSES)]
+        plane = tile([P, T // 4], I32, "plane")
+
+        w_rows = w.rearrange("(p j) r -> p j r", j=PACK)
+        x_rows = x.rearrange("(p j) m -> p j m", j=PACK)
+
+        warm = tile([P, 8], F32, "warm")
+        warm_out = tile([P, 8], F32, "warm_out")
+        nc.vector.memset(plane[:], 0)
+        nc.vector.memset(warm[:], 0.0)
+        nc.scalar.activation(warm_out[:], warm[:], TANH)
+
+        def load_x(h):
+            nc.sync.dma_start(out=x_raw[h][:], in_=x_rows[:, :, h * XW : (h + 1) * XW])
+
+        def load_words(a):
+            nc.sync.dma_start(out=words[a][:], in_=tab_words[a].rearrange("p t i -> p (t i)").bitcast(I32))
+
+        nc.sync.dma_start(out=w_raw[0][:], in_=w_rows[:, :, 0:512])
+        nc.sync.dma_start(out=w_raw[1][:], in_=w_rows[:, :, 512:1024])
+        scale_rows = tab_scales.bitcast(I32)
+
+        def load_scales(a):
+            for q in range(4):
+                row = 32 * q + 4 * a
+                nc.sync.dma_start(out=plane[row : row + 4, :], in_=scale_rows[a, 4 * q : 4 * q + 4, :])
+
+        load_scales(0)
+        nc.sync.dma_start(offsets[:], offs)
+        load_x(0)
+        load_scales(1)
+        load_words(0)
+        load_words(1)
+        load_x(1)
+        nc.sync.dma_start(
+            out=wv_raw[:].rearrange("p a j n -> p a (j n)"),
+            in_=wv.rearrange("(a p j) n -> p a (j n)", a=PASSES, j=PACK),
+        )
+
+        def quantize(src, width, name):
+            codes = tile([P, width // 4], U32, name + "_codes")
+            scales = tile([P, width // 4], U8, name + "_scales")
+            nc.vector.quantize_mx(out=codes[:].bitcast(FP8X4), scales=scales[:], in_=src)
+            return codes, scales
+
+        def copy_on(engine, out, in_):
+            if engine == "s":
+                nc.scalar.copy(out, in_)
+            else:
+                nc.vector.tensor_copy(out, in_)
+
+        def cast_w(a, engine):
+            wb = tile([P, 2048], BF16, "w_bf%d" % a)
+            copy_on(
+                engine,
+                wb[:].rearrange("p (t m j) -> p m t j", t=4, j=4),
+                w_raw[a][:].rearrange("p j (m t) -> p m t j", t=4),
+            )
+            return wb
+
+        def interleave(engine, dst, src):
+            copy_on(
+                engine,
+                dst.rearrange("p (c i j) -> p c j i", i=4, j=4),
+                src.rearrange("p j (c i) -> p c j i", i=4),
+            )
+
+        def cast_x(h, engine):
+            xb = tile([P, 4 * XW], BF16, "x_bf%d" % h)
+            interleave(engine, xb[:], x_raw[h][:])
+            return xb
+
+        def gather(src, dtype, j, name):
+            got = tile([P, JW], dtype, name)
+            cols = slice(j * JW // 16, (j + 1) * JW // 16)
+            nc.vector.tensor_copy(got[:], src[:].bitcast(dtype).indirect(offsets[:, cols]))
+            return got
+
+        def mm(out, lhs, lhs_cols, rhs, rhs_scale, start, stop):
+            nc.tensor.matmul_mx(
+                out=out,
+                lhsT=lhs[0][:, lhs_cols].bitcast(FP8X4),
+                lhsT_scale=lhs[1][:, lhs_cols],
+                rhs=rhs.bitcast(FP8X4),
+                rhs_scale=rhs_scale,
+                start=start,
+                stop=stop,
+            )
+
+        wq = [None, None]
+        xq = [None] * (M // XW)
+        qa = [None] * (M // P)
+        gw = {}
+        gs = {}
+
+        def make_qa(mt, engine):
+            h, c0 = divmod(mt * P, XW)
+            qb = tile([P, PASSES, P, PACK], BF16, "qa_bf%d" % mt)
+            for a in range(PASSES):
+                bank = qa_psum.tile([P, PACK, P], F32, name="qa_bank")
+                for t in range(PACK):
+                    mm(bank[:, t, :], wq[a], slice(t * P, (t + 1) * P),
+                       xq[h][0][:, c0 : c0 + P], xq[h][1][:, c0 : c0 + P], True, True)
+                copy_on(engine, qb[:, a, :, :], bank[:].rearrange("p t m -> p m t"))
+            return qb
+
+        def quant_qa(mt, qb):
+            qa[mt] = quantize(qb[:].rearrange("p a m t -> p (a m t)"), 1024, "qa%d" % mt)
+
+        def product(lhs, c0, stride, j):
+            bank = psum.tile([P, JW], F32, name="bank")
+            for a in range(PASSES):
+                mm(bank[:], lhs, slice(a * stride + c0, a * stride + c0 + P),
+                   gw[a, j][:], gs[j][4 * a : P, :], a == 0, a == PASSES - 1)
+            return bank
+
+        capped = [tile([P, J], F32, "capped%d" % mt) for mt in range(M // P)]
+        values = [tile([P, J], F32, "values%d" % nt) for nt in range(N // P)]
+
+        def score(mt, j):
+            bank = product(qa[mt], 0, P, j)
+            nc.scalar.activation(capped[mt][:, j * JW : (j + 1) * JW], bank[:], TANH, scale=0.00390625)
+
+        def times8(mt, j0, j1):
+            cols = slice(j0 * JW, j1 * JW)
+            nc.vector.tensor_scalar(capped[mt][:, cols], capped[mt][:, cols], 8.0, None, MULT)
+
+        def store0(mt, j0, j1):
+            cols = slice(j0 * JW, j1 * JW)
+            nc.sync.dma_start(out=out_0[mt * P : (mt + 1) * P, cols], in_=capped[mt][:, cols])
+
+        def value(nt, j, engine):
+            bank = product(wvq, nt * P, N, j)
+            copy_on(engine, values[nt][:, j * JW : (j + 1) * JW], bank[:])
+
+        wb0 = cast_w(0, "s")
+        wb1 = cast_w(1, "v")
+        wq[0] = quantize(wb0[:], 2048, "w0")
+        xb0 = cast_x(0, "s")
+        wq[1] = quantize(wb1[:], 2048, "w1")
+        xq[0] = quantize(xb0[:], 2048, "x0")
+        for mt in range(4):
+            quant_qa(mt, make_qa(mt, "s"))
+        for j in range(NJ):
+            gs[j] = gather(plane, U8, j, "gs%d" % j)
+        for j in range(NJ):
+            gw[0, j] = gather(words[0], U32, j, "gw0%d" % j)
+        for j in range(2):
+            gw[1, j] = gather(words[1], U32, j, "gw1%d" % j)
+
+        for mt in range(4):
+            if mt == 2:
+                for j in range(2, 4):
+                    gw[1, j] = gather(words[1], U32, j, "gw1%d" % j)
+                xb1 = cast_x(1, "v")
+            for j in range(2):
+                score(mt, j)
+            times8(mt, 0, 2)
+            store0(mt, 0, 2)
+        xq[1] = quantize(xb1[:], 2048, "x1")
+        wvb = tile([P, PASSES, 4 * N], BF16, "wv_bf")
+        for mt in range(4):
+            qb = make_qa(4 + mt, "v" if mt % 2 == 0 else "s")
+            for j in range(2, 4):
+                score(mt, j)
+            quant_qa(4 + mt, qb)
+            times8(mt, 2, 4)
+            store0(mt, 2, 4)
+            if mt < 2:
+                interleave("v", wvb[:, mt, :], wv_raw[:, mt, :, :])
+        wvq = quantize(wvb[:].rearrange("p a c -> p (a c)"), 2048, "wv")
+        for mt in range(4, 8):
+            nt, jv = divmod(2 * (mt - 4), NJ)
+            for j in range(NJ):
+                score(mt, j)
+                if j % 2 == 1:
+                    times8(mt, j - 1, j + 1)
+                    if mt == 7:
+                        store0(mt, j - 1, j + 1)
+                else:
+                    value(nt, jv + j // 2, "v")
+            if mt < 7:
+                store0(mt, 0, 4)
+            if jv == 2:
+                nc.sync.dma_start(out=out_1[nt * P : (nt + 1) * P, :], in_=values[nt][:])

@@ -14,13 +14,14 @@ U8 = mybir.dt.uint8
 FP8X4 = mybir.dt.float8_e4m3fn_x4
 TANH = mybir.ActivationFunctionType.Tanh
 MULT = mybir.AluOpType.mult
+ADD = mybir.AluOpType.add
 
 P = 128
 PACK = 4
 PASSES = 2
 JW = 512
-NJ = J // JW
-XW = 512
+SCALE_ROW = (0, 4)
+X_PIECES = [(0, 512), (512, 1024)]
 
 
 def tile_list_mlat_cap_kernel(tc, x, w, tab_words, tab_scales, wv, offs, out_0, out_1):
@@ -35,46 +36,47 @@ def tile_list_mlat_cap_kernel(tc, x, w, tab_words, tab_scales, wv, offs, out_0, 
 
         offsets = keep.tile([P, J // 16], U16, name="offsets")
         w_raw = [tile([P, PACK, 512], F32, "w_raw%d" % a) for a in range(PASSES)]
-        x_raw = [tile([P, PACK, XW], F32, "x_raw%d" % h) for h in range(M // XW)]
+        x_raw = [tile([P, PACK, hi - lo], F32, "x_raw%d" % lo) for lo, hi in X_PIECES]
         wv_raw = tile([P, PASSES, PACK, N], F32, "wv_raw")
         words = [tile([P, T], I32, "words%d" % a) for a in range(PASSES)]
         plane = tile([P, T // 4], I32, "plane")
+        w_bf = [tile([P, 2048], BF16, "w_bf%d" % a) for a in range(PASSES)]
+        x_bf = [tile([P, 4 * (hi - lo)], BF16, "x_bf%d" % lo) for lo, hi in X_PIECES]
+        wv_bf = tile([P, PASSES, 4 * N], BF16, "wv_bf")
+        qa_bf = [tile([P, PASSES, P, PACK], BF16, "qa_bf%d" % mt) for mt in range(M // P)]
+        capped = [tile([P, J], F32, "capped%d" % mt) for mt in range(M // P)]
+        values = [tile([P, J], F32, "values%d" % nt) for nt in range(N // P)]
 
         w_rows = w.rearrange("(p j) r -> p j r", j=PACK)
         x_rows = x.rearrange("(p j) m -> p j m", j=PACK)
+        scale_rows = tab_scales.bitcast(I32)
 
-        warm = tile([P, 8], F32, "warm")
-        warm_out = tile([P, 8], F32, "warm_out")
+        zero = tile([P, 1], F32, "zero")
+        bias = tile([P, 1], F32, "bias")
         nc.vector.memset(plane[:], 0)
-        nc.vector.memset(warm[:], 0.0)
-        nc.scalar.activation(warm_out[:], warm[:], TANH)
+        nc.vector.memset(zero[:], 0.0)
+        nc.scalar.activation(bias[:], zero[:], TANH)
+
+        def load_offsets():
+            nc.sync.dma_start(offsets[:], offs)
+
+        def load_w(a):
+            nc.sync.dma_start(out=w_raw[a][:], in_=w_rows[:, :, 512 * a : 512 * (a + 1)])
 
         def load_x(h):
-            nc.sync.dma_start(out=x_raw[h][:], in_=x_rows[:, :, h * XW : (h + 1) * XW])
+            nc.sync.dma_start(out=x_raw[h][:], in_=x_rows[:, :, X_PIECES[h][0] : X_PIECES[h][1]])
 
         def load_words(a):
             nc.sync.dma_start(out=words[a][:], in_=tab_words[a].rearrange("p t i -> p (t i)").bitcast(I32))
 
-        nc.sync.dma_start(out=w_raw[0][:], in_=w_rows[:, :, 0:512])
-        nc.sync.dma_start(out=w_raw[1][:], in_=w_rows[:, :, 512:1024])
-        scale_rows = tab_scales.bitcast(I32)
+        def load_wv():
+            nc.sync.dma_start(
+                out=wv_raw[:].rearrange("p a j n -> p a (j n)"),
+                in_=wv.rearrange("(a p j) n -> p a (j n)", a=PASSES, j=PACK),
+            )
 
-        def load_scales(a):
-            for q in range(4):
-                row = 32 * q + 4 * a
-                nc.sync.dma_start(out=plane[row : row + 4, :], in_=scale_rows[a, 4 * q : 4 * q + 4, :])
-
-        load_scales(0)
-        nc.sync.dma_start(offsets[:], offs)
-        load_x(0)
-        load_scales(1)
-        load_words(0)
-        load_words(1)
-        load_x(1)
-        nc.sync.dma_start(
-            out=wv_raw[:].rearrange("p a j n -> p a (j n)"),
-            in_=wv.rearrange("(a p j) n -> p a (j n)", a=PASSES, j=PACK),
-        )
+        def load_scales(q):
+            nc.gpsimd.dma_start(out=plane[32 * q : 32 * q + 8, :], in_=scale_rows[:, 4 * q : 4 * q + 4, :])
 
         def quantize(src, width, name):
             codes = tile([P, width // 4], U32, name + "_codes")
@@ -85,17 +87,27 @@ def tile_list_mlat_cap_kernel(tc, x, w, tab_words, tab_scales, wv, offs, out_0, 
         def copy_on(engine, out, in_):
             if engine == "s":
                 nc.scalar.copy(out, in_)
-            else:
+            elif engine == "v":
                 nc.vector.tensor_copy(out, in_)
+            else:
+                nc.gpsimd.tensor_scalar(out, in_, 1.0, 0.0, MULT, ADD)
 
-        def cast_w(a, engine):
-            wb = tile([P, 2048], BF16, "w_bf%d" % a)
+        wq = {}
+        xq = {}
+        qa = {}
+        wvq = {}
+        gw = {}
+        gs = {}
+
+        def cast_w(a, engine, m0=0, m1=P):
             copy_on(
                 engine,
-                wb[:].rearrange("p (t m j) -> p m t j", t=4, j=4),
-                w_raw[a][:].rearrange("p j (m t) -> p m t j", t=4),
+                w_bf[a][:].rearrange("p (t m j) -> p m t j", t=4, j=4)[:, m0:m1],
+                w_raw[a][:].rearrange("p j (m t) -> p m t j", t=4)[:, m0:m1],
             )
-            return wb
+
+        def quant_w(a):
+            wq[a] = quantize(w_bf[a][:], 2048, "w%d" % a)
 
         def interleave(engine, dst, src):
             copy_on(
@@ -104,16 +116,32 @@ def tile_list_mlat_cap_kernel(tc, x, w, tab_words, tab_scales, wv, offs, out_0, 
                 src.rearrange("p j (c i) -> p c j i", i=4),
             )
 
-        def cast_x(h, engine):
-            xb = tile([P, 4 * XW], BF16, "x_bf%d" % h)
-            interleave(engine, xb[:], x_raw[h][:])
-            return xb
+        def cast_x(h, engine, c0=0, c1=None):
+            c1 = c1 or X_PIECES[h][1] - X_PIECES[h][0]
+            interleave(engine, x_bf[h][:, 4 * c0 : 4 * c1], x_raw[h][:, :, c0:c1])
 
-        def gather(src, dtype, j, name):
-            got = tile([P, JW], dtype, name)
-            cols = slice(j * JW // 16, (j + 1) * JW // 16)
+        def quant_x(h):
+            xq[h] = quantize(x_bf[h][:], 4 * (X_PIECES[h][1] - X_PIECES[h][0]), "x%d" % h)
+
+        def cast_wv(a, engine):
+            interleave(engine, wv_bf[:, a, :], wv_raw[:, a, :, :])
+
+        def quant_wv():
+            wvq[0] = quantize(wv_bf[:].rearrange("p a c -> p (a c)"), 2048, "wv")
+
+        def gather(src, dtype, j, n, name):
+            got = tile([P, n * JW], dtype, name)
+            cols = slice(j * JW // 16, (j + n) * JW // 16)
             nc.vector.tensor_copy(got[:], src[:].bitcast(dtype).indirect(offsets[:, cols]))
-            return got
+            return [got[:, i * JW : (i + 1) * JW] for i in range(n)]
+
+        def gather_s(j, n=1):
+            for i, got in enumerate(gather(plane, U8, j, n, "gs%d" % j)):
+                gs[j + i] = got
+
+        def gather_w(a, j, n=1):
+            for i, got in enumerate(gather(words[a], U32, j, n, "gw%d%d" % (a, j))):
+                gw[a, j + i] = got
 
         def mm(out, lhs, lhs_cols, rhs, rhs_scale, start, stop):
             nc.tensor.matmul_mx(
@@ -126,99 +154,142 @@ def tile_list_mlat_cap_kernel(tc, x, w, tab_words, tab_scales, wv, offs, out_0, 
                 stop=stop,
             )
 
-        wq = [None, None]
-        xq = [None] * (M // XW)
-        qa = [None] * (M // P)
-        gw = {}
-        gs = {}
+        def make_qa(mt, a, engine):
+            h = [i for i, (lo, hi) in enumerate(X_PIECES) if lo <= mt * P < hi][0]
+            c0 = mt * P - X_PIECES[h][0]
+            bank = qa_psum.tile([P, PACK, P], F32, name="qa_bank")
+            for t in range(PACK):
+                mm(bank[:, t, :], wq[a], slice(t * P, (t + 1) * P),
+                   xq[h][0][:, c0 : c0 + P], xq[h][1][:, c0 : c0 + P], True, True)
+            copy_on(engine, qa_bf[mt][:, a, :, :], bank[:].rearrange("p t m -> p m t"))
 
-        def make_qa(mt, engine):
-            h, c0 = divmod(mt * P, XW)
-            qb = tile([P, PASSES, P, PACK], BF16, "qa_bf%d" % mt)
-            for a in range(PASSES):
-                bank = qa_psum.tile([P, PACK, P], F32, name="qa_bank")
-                for t in range(PACK):
-                    mm(bank[:, t, :], wq[a], slice(t * P, (t + 1) * P),
-                       xq[h][0][:, c0 : c0 + P], xq[h][1][:, c0 : c0 + P], True, True)
-                copy_on(engine, qb[:, a, :, :], bank[:].rearrange("p t m -> p m t"))
-            return qb
-
-        def quant_qa(mt, qb):
-            qa[mt] = quantize(qb[:].rearrange("p a m t -> p (a m t)"), 1024, "qa%d" % mt)
+        def quant_qa(mt):
+            qa[mt] = quantize(qa_bf[mt][:].rearrange("p a m t -> p (a m t)"), 1024, "qa%d" % mt)
 
         def product(lhs, c0, stride, j):
             bank = psum.tile([P, JW], F32, name="bank")
             for a in range(PASSES):
                 mm(bank[:], lhs, slice(a * stride + c0, a * stride + c0 + P),
-                   gw[a, j][:], gs[j][4 * a : P, :], a == 0, a == PASSES - 1)
+                   gw[a, j], gs[j][SCALE_ROW[a] : P, :], a == 0, a == PASSES - 1)
             return bank
-
-        capped = [tile([P, J], F32, "capped%d" % mt) for mt in range(M // P)]
-        values = [tile([P, J], F32, "values%d" % nt) for nt in range(N // P)]
 
         def score(mt, j):
             bank = product(qa[mt], 0, P, j)
-            nc.scalar.activation(capped[mt][:, j * JW : (j + 1) * JW], bank[:], TANH, scale=0.00390625)
+            nc.scalar.activation(capped[mt][:, j * JW : (j + 1) * JW], bank[:], TANH, bias=bias[:], scale=0.00390625)
 
-        def times8(mt, j0, j1):
+        def times8(mt, j0, j1, engine):
             cols = slice(j0 * JW, j1 * JW)
-            nc.vector.tensor_scalar(capped[mt][:, cols], capped[mt][:, cols], 8.0, None, MULT)
+            if engine == "v":
+                nc.vector.tensor_scalar(capped[mt][:, cols], capped[mt][:, cols], 8.0, None, MULT)
+            else:
+                nc.gpsimd.tensor_scalar(capped[mt][:, cols], capped[mt][:, cols], 8.0, 0.0, MULT, ADD)
 
         def store0(mt, j0, j1):
             cols = slice(j0 * JW, j1 * JW)
             nc.sync.dma_start(out=out_0[mt * P : (mt + 1) * P, cols], in_=capped[mt][:, cols])
 
         def value(nt, j, engine):
-            bank = product(wvq, nt * P, N, j)
+            bank = product(wvq[0], nt * P, N, j)
             copy_on(engine, values[nt][:, j * JW : (j + 1) * JW], bank[:])
 
-        wb0 = cast_w(0, "s")
-        wb1 = cast_w(1, "v")
-        wq[0] = quantize(wb0[:], 2048, "w0")
-        xb0 = cast_x(0, "s")
-        wq[1] = quantize(wb1[:], 2048, "w1")
-        xq[0] = quantize(xb0[:], 2048, "x0")
-        for mt in range(4):
-            quant_qa(mt, make_qa(mt, "s"))
-        for j in range(NJ):
-            gs[j] = gather(plane, U8, j, "gs%d" % j)
-        for j in range(NJ):
-            gw[0, j] = gather(words[0], U32, j, "gw0%d" % j)
-        for j in range(2):
-            gw[1, j] = gather(words[1], U32, j, "gw1%d" % j)
+        def store1(nt, j0, j1):
+            cols = slice(j0 * JW, j1 * JW)
+            nc.sync.dma_start(out=out_1[nt * P : (nt + 1) * P, cols], in_=values[nt][:, cols])
 
-        for mt in range(4):
-            if mt == 2:
-                for j in range(2, 4):
-                    gw[1, j] = gather(words[1], U32, j, "gw1%d" % j)
-                xb1 = cast_x(1, "v")
-            for j in range(2):
+        def part(mt, j0, j1, engine):
+            for j in range(j0, j1):
                 score(mt, j)
-            times8(mt, 0, 2)
-            store0(mt, 0, 2)
-        xq[1] = quantize(xb1[:], 2048, "x1")
-        wvb = tile([P, PASSES, 4 * N], BF16, "wv_bf")
-        for mt in range(4):
-            qb = make_qa(4 + mt, "v" if mt % 2 == 0 else "s")
-            for j in range(2, 4):
-                score(mt, j)
-            quant_qa(4 + mt, qb)
-            times8(mt, 2, 4)
-            store0(mt, 2, 4)
-            if mt < 2:
-                interleave("v", wvb[:, mt, :], wv_raw[:, mt, :, :])
-        wvq = quantize(wvb[:].rearrange("p a c -> p (a c)"), 2048, "wv")
-        for mt in range(4, 8):
-            nt, jv = divmod(2 * (mt - 4), NJ)
-            for j in range(NJ):
-                score(mt, j)
-                if j % 2 == 1:
-                    times8(mt, j - 1, j + 1)
-                    if mt == 7:
-                        store0(mt, j - 1, j + 1)
-                else:
-                    value(nt, jv + j // 2, "v")
-            if mt < 7:
-                store0(mt, 0, 4)
-            if jv == 2:
-                nc.sync.dma_start(out=out_1[nt * P : (nt + 1) * P, :], in_=values[nt][:])
+            times8(mt, j0, j1, engine)
+            store0(mt, j0, j1)
+
+        load_x(0)
+        load_offsets()
+        load_scales(0)
+        load_scales(1)
+        load_scales(2)
+        load_scales(3)
+        load_w(0)
+        load_w(1)
+        load_words(0)
+        load_words(1)
+        load_x(1)
+        load_wv()
+        cast_x(0, "v")
+        gather_w(0, 0)
+        cast_x(1, "s")
+        gather_s(1)
+        gather_s(3)
+        quant_x(0)
+        cast_wv(1, "v")
+        gather_w(0, 2)
+        gather_w(1, 0)
+        gather_w(0, 3)
+        cast_w(1, "s")
+        cast_w(0, "s")
+        quant_w(0)
+        make_qa(2, 0, "s")
+        make_qa(1, 0, "s")
+        make_qa(3, 0, "s")
+        gather_s(0)
+        quant_x(1)
+        gather_w(1, 1)
+        make_qa(0, 0, "s")
+        gather_w(0, 1)
+        quant_w(1)
+        make_qa(3, 1, "s")
+        quant_qa(3)
+        part(3, 1, 2, "v")
+        make_qa(1, 1, "s")
+        quant_qa(1)
+        part(1, 0, 1, "v")
+        make_qa(0, 1, "s")
+        quant_qa(0)
+        part(3, 0, 1, "v")
+        make_qa(4, 1, "v")
+        make_qa(2, 1, "s")
+        quant_qa(2)
+        part(2, 1, 2, "v")
+        part(2, 0, 1, "v")
+        make_qa(5, 1, "s")
+        part(0, 0, 1, "v")
+        part(1, 1, 2, "v")
+        cast_wv(0, "v")
+        gather_w(1, 3)
+        gather_w(1, 2)
+        make_qa(4, 0, "v")
+        quant_qa(4)
+        gather_s(2)
+        part(1, 2, 4, "v")
+        make_qa(5, 0, "v")
+        quant_qa(5)
+        part(0, 1, 2, "v")
+        part(0, 2, 4, "v")
+        part(3, 2, 4, "v")
+        part(2, 2, 4, "v")
+        make_qa(6, 0, "v")
+        part(4, 2, 4, "v")
+        quant_wv()
+        part(4, 0, 2, "v")
+        make_qa(6, 1, "v")
+        make_qa(7, 1, "s")
+        quant_qa(6)
+        value(1, 3, "v")
+        make_qa(7, 0, "s")
+        quant_qa(7)
+        part(5, 0, 2, "v")
+        value(0, 1, "v")
+        value(0, 0, "s")
+        store1(0, 0, 2)
+        value(1, 0, "v")
+        value(1, 1, "v")
+        store1(1, 0, 2)
+        part(6, 0, 2, "v")
+        part(6, 2, 4, "v")
+        part(7, 0, 2, "v")
+        part(5, 2, 4, "v")
+        value(0, 2, "v")
+        value(1, 2, "s")
+        store1(1, 2, 4)
+        value(0, 3, "v")
+        store1(0, 2, 4)
+        part(7, 2, 4, "v")

@@ -13,6 +13,7 @@ U16 = mybir.dt.uint16
 U8 = mybir.dt.uint8
 FP8X4 = mybir.dt.float8_e4m3fn_x4
 TANH = mybir.ActivationFunctionType.Tanh
+COPY = mybir.ActivationFunctionType.Copy
 MULT = mybir.AluOpType.mult
 ADD = mybir.AluOpType.add
 
@@ -28,32 +29,37 @@ def tile_list_mlat_cap_kernel(tc, x, w, tab_words, tab_scales, wv, offs, out_0, 
     nc = tc.nc
     with ExitStack() as ctx:
         keep = ctx.enter_context(tc.tile_pool(name="keep", bufs=1))
-        qa_psum = ctx.enter_context(tc.psum_pool(name="qa_psum", bufs=2))
-        psum = ctx.enter_context(tc.psum_pool(name="psum", bufs=6))
+        psum = ctx.enter_context(tc.psum_pool(name="psum", bufs=8))
+        early = ctx.enter_context(tc.tile_pool(name="early", bufs=15))
+        late = ctx.enter_context(tc.tile_pool(name="late", bufs=22))
 
-        def tile(shape, dtype, name):
-            return keep.tile(shape, dtype, name=name, align_bytes=64)
+        def tile(shape, dtype, name, tag=None):
+            if tag == "late":
+                return late.tile(shape, dtype, name=name, tag=tag, align_bytes=64)
+            if tag == "early":
+                return early.tile(shape, dtype, name=name, tag=tag, align_bytes=64)
+            return keep.tile(shape, dtype, name=name, tag=tag or name, align_bytes=64)
 
         offsets = keep.tile([P, J // 16], U16, name="offsets")
         w_raw = [tile([P, PACK, 512], F32, "w_raw%d" % a) for a in range(PASSES)]
         x_raw = [tile([P, PACK, hi - lo], F32, "x_raw%d" % lo) for lo, hi in X_PIECES]
-        wv_raw = tile([P, PASSES, PACK, N], F32, "wv_raw")
         words = [tile([P, T], I32, "words%d" % a) for a in range(PASSES)]
         plane = tile([P, T // 4], I32, "plane")
         w_bf = [tile([P, 2048], BF16, "w_bf%d" % a) for a in range(PASSES)]
         x_bf = [tile([P, 4 * (hi - lo)], BF16, "x_bf%d" % lo) for lo, hi in X_PIECES]
-        wv_bf = tile([P, PASSES, 4 * N], BF16, "wv_bf")
-        qa_bf = [tile([P, PASSES, P, PACK], BF16, "qa_bf%d" % mt) for mt in range(M // P)]
-        capped = [tile([P, J], F32, "capped%d" % mt) for mt in range(M // P)]
-        values = [tile([P, J], F32, "values%d" % nt) for nt in range(N // P)]
+        qa_bf = {}
+        values = {}
+        held = {}
 
         w_rows = w.rearrange("(p j) r -> p j r", j=PACK)
         x_rows = x.rearrange("(p j) m -> p j m", j=PACK)
+        out_rows = out_0.rearrange("(mt p) j -> p mt j", p=P)
         scale_rows = tab_scales.bitcast(I32)
 
         zero = tile([P, 1], F32, "zero")
         bias = tile([P, 1], F32, "bias")
-        nc.vector.memset(plane[:], 0)
+        nc.vector.memset(plane[:, : T // 8], 0)
+        nc.gpsimd.memset(plane[:, T // 8 :], 0)
         nc.vector.memset(zero[:], 0.0)
         nc.scalar.activation(bias[:], zero[:], TANH)
 
@@ -70,16 +76,17 @@ def tile_list_mlat_cap_kernel(tc, x, w, tab_words, tab_scales, wv, offs, out_0, 
             nc.sync.dma_start(out=words[a][:], in_=tab_words[a].rearrange("p t i -> p (t i)").bitcast(I32))
 
         def load_wv():
+            held["wv"] = tile([P, PASSES, PACK, N], F32, "wv_raw", "x_raw0")
             nc.sync.dma_start(
-                out=wv_raw[:].rearrange("p a j n -> p a (j n)"),
+                out=held["wv"][:].rearrange("p a j n -> p a (j n)"),
                 in_=wv.rearrange("(a p j) n -> p a (j n)", a=PASSES, j=PACK),
             )
 
         def load_scales(q):
-            nc.gpsimd.dma_start(out=plane[32 * q : 32 * q + 8, :], in_=scale_rows[:, 4 * q : 4 * q + 4, :])
+            nc.sync.dma_start(out=plane[32 * q : 32 * q + 8, :], in_=scale_rows[:, 4 * q : 4 * q + 4, :])
 
-        def quantize(src, width, name):
-            codes = tile([P, width // 4], U32, name + "_codes")
+        def quantize(src, width, name, tag):
+            codes = tile([P, width // 4], U32, name + "_codes", tag)
             scales = tile([P, width // 4], U8, name + "_scales")
             nc.vector.quantize_mx(out=codes[:].bitcast(FP8X4), scales=scales[:], in_=src)
             return codes, scales
@@ -106,8 +113,8 @@ def tile_list_mlat_cap_kernel(tc, x, w, tab_words, tab_scales, wv, offs, out_0, 
                 w_raw[a][:].rearrange("p j (m t) -> p m t j", t=4)[:, m0:m1],
             )
 
-        def quant_w(a):
-            wq[a] = quantize(w_bf[a][:], 2048, "w%d" % a)
+        def quant_w(a, tag):
+            wq[a] = quantize(w_bf[a][:], 2048, "w%d" % a, tag)
 
         def interleave(engine, dst, src):
             copy_on(
@@ -120,27 +127,29 @@ def tile_list_mlat_cap_kernel(tc, x, w, tab_words, tab_scales, wv, offs, out_0, 
             c1 = c1 or X_PIECES[h][1] - X_PIECES[h][0]
             interleave(engine, x_bf[h][:, 4 * c0 : 4 * c1], x_raw[h][:, :, c0:c1])
 
-        def quant_x(h):
-            xq[h] = quantize(x_bf[h][:], 4 * (X_PIECES[h][1] - X_PIECES[h][0]), "x%d" % h)
+        def quant_x(h, tag):
+            xq[h] = quantize(x_bf[h][:], 4 * (X_PIECES[h][1] - X_PIECES[h][0]), "x%d" % h, tag)
 
         def cast_wv(a, engine):
-            interleave(engine, wv_bf[:, a, :], wv_raw[:, a, :, :])
+            if "wv_bf" not in held:
+                held["wv_bf"] = tile([P, PASSES, 4 * N], BF16, "wv_bf", "x_bf0")
+            interleave(engine, held["wv_bf"][:, a, :], held["wv"][:, a, :, :])
 
-        def quant_wv():
-            wvq[0] = quantize(wv_bf[:].rearrange("p a c -> p (a c)"), 2048, "wv")
+        def quant_wv(tag):
+            wvq[0] = quantize(held["wv_bf"][:].rearrange("p a c -> p (a c)"), 2048, "wv", tag)
 
-        def gather(src, dtype, j, n, name):
-            got = tile([P, n * JW], dtype, name)
+        def gather(src, dtype, j, n, name, tag=None):
+            got = tile([P, n * JW], dtype, name, tag)
             cols = slice(j * JW // 16, (j + n) * JW // 16)
             nc.vector.tensor_copy(got[:], src[:].bitcast(dtype).indirect(offsets[:, cols]))
             return [got[:, i * JW : (i + 1) * JW] for i in range(n)]
 
-        def gather_s(j, n=1):
-            for i, got in enumerate(gather(plane, U8, j, n, "gs%d" % j)):
+        def gather_s(j, n=1, tag=None):
+            for i, got in enumerate(gather(plane, U8, j, n, "gs%d" % j, tag)):
                 gs[j + i] = got
 
-        def gather_w(a, j, n=1):
-            for i, got in enumerate(gather(words[a], U32, j, n, "gw%d%d" % (a, j))):
+        def gather_w(a, j, n=1, tag=None):
+            for i, got in enumerate(gather(words[a], U32, j, n, "gw%d%d" % (a, j), tag)):
                 gw[a, j + i] = got
 
         def mm(out, lhs, lhs_cols, rhs, rhs_scale, start, stop):
@@ -157,14 +166,16 @@ def tile_list_mlat_cap_kernel(tc, x, w, tab_words, tab_scales, wv, offs, out_0, 
         def make_qa(mt, a, engine):
             h = [i for i, (lo, hi) in enumerate(X_PIECES) if lo <= mt * P < hi][0]
             c0 = mt * P - X_PIECES[h][0]
-            bank = qa_psum.tile([P, PACK, P], F32, name="qa_bank")
+            if mt not in qa_bf:
+                qa_bf[mt] = tile([P, PASSES, P, PACK], BF16, "qa_bf%d" % mt, "qa_bf%d" % (mt % 4))
+            bank = psum.tile([P, PACK, P], F32, name="bank")
             for t in range(PACK):
                 mm(bank[:, t, :], wq[a], slice(t * P, (t + 1) * P),
                    xq[h][0][:, c0 : c0 + P], xq[h][1][:, c0 : c0 + P], True, True)
             copy_on(engine, qa_bf[mt][:, a, :, :], bank[:].rearrange("p t m -> p m t"))
 
-        def quant_qa(mt):
-            qa[mt] = quantize(qa_bf[mt][:].rearrange("p a m t -> p (a m t)"), 1024, "qa%d" % mt)
+        def quant_qa(mt, tag):
+            qa[mt] = quantize(qa_bf[mt][:].rearrange("p a m t -> p (a m t)"), 1024, "qa%d" % mt, tag)
 
         def product(lhs, c0, stride, j):
             bank = psum.tile([P, JW], F32, name="bank")
@@ -173,34 +184,31 @@ def tile_list_mlat_cap_kernel(tc, x, w, tab_words, tab_scales, wv, offs, out_0, 
                    gw[a, j], gs[j][SCALE_ROW[a] : P, :], a == 0, a == PASSES - 1)
             return bank
 
-        def score(mt, j):
-            bank = product(qa[mt], 0, P, j)
-            nc.scalar.activation(capped[mt][:, j * JW : (j + 1) * JW], bank[:], TANH, bias=bias[:], scale=0.00390625)
-
-        def times8(mt, j0, j1, engine):
-            cols = slice(j0 * JW, j1 * JW)
+        def block(m0, m1, j0, j1, engine):
+            capped = late.tile([P, m1 - m0, (j1 - j0) * JW], F32, name="capped%d%d" % (m0, j0), tag="late", align_bytes=64)
+            for mt in range(m0, m1):
+                for j in range(j0, j1):
+                    bank = product(qa[mt], 0, P, j)
+                    nc.scalar.activation(capped[:, mt - m0, (j - j0) * JW : (j - j0 + 1) * JW], bank[:], TANH, bias=bias[:], scale=0.00390625)
             if engine == "v":
-                nc.vector.tensor_scalar(capped[mt][:, cols], capped[mt][:, cols], 8.0, None, MULT)
+                nc.vector.tensor_scalar(capped[:], capped[:], 8.0, None, MULT)
+            elif engine == "s":
+                nc.scalar.activation(capped[:], capped[:], COPY, scale=8.0)
             else:
-                nc.gpsimd.tensor_scalar(capped[mt][:, cols], capped[mt][:, cols], 8.0, 0.0, MULT, ADD)
-
-        def store0(mt, j0, j1):
-            cols = slice(j0 * JW, j1 * JW)
-            nc.sync.dma_start(out=out_0[mt * P : (mt + 1) * P, cols], in_=capped[mt][:, cols])
+                nc.gpsimd.tensor_scalar(capped[:], capped[:], 8.0, 0.0, MULT, ADD)
+            nc.sync.dma_start(out=out_rows[:, m0:m1, j0 * JW : j1 * JW], in_=capped[:])
 
         def value(nt, j, engine):
+            key = (nt, j // 2)
+            if key not in values:
+                tag = (("w_bf0", "w_raw1"), ("w_bf1", "x_raw%d" % X_PIECES[-1][0]))[nt][j // 2]
+                values[key] = tile([P, 2 * JW], F32, "values%d%d" % key, tag)
             bank = product(wvq[0], nt * P, N, j)
-            copy_on(engine, values[nt][:, j * JW : (j + 1) * JW], bank[:])
+            copy_on(engine, values[key][:, (j % 2) * JW : (j % 2 + 1) * JW], bank[:])
 
         def store1(nt, j0, j1):
             cols = slice(j0 * JW, j1 * JW)
-            nc.sync.dma_start(out=out_1[nt * P : (nt + 1) * P, cols], in_=values[nt][:, cols])
-
-        def part(mt, j0, j1, engine):
-            for j in range(j0, j1):
-                score(mt, j)
-            times8(mt, j0, j1, engine)
-            store0(mt, j0, j1)
+            nc.sync.dma_start(out=out_1[nt * P : (nt + 1) * P, cols], in_=values[nt, j0 // 2][:])
 
         load_x(0)
         load_offsets()
@@ -213,83 +221,81 @@ def tile_list_mlat_cap_kernel(tc, x, w, tab_words, tab_scales, wv, offs, out_0, 
         load_words(0)
         load_words(1)
         load_x(1)
-        load_wv()
         cast_x(0, "v")
-        gather_w(0, 0)
-        cast_x(1, "s")
-        gather_s(1)
-        gather_s(3)
-        quant_x(0)
-        cast_wv(1, "v")
-        gather_w(0, 2)
-        gather_w(1, 0)
-        gather_w(0, 3)
+        load_wv()
+        quant_x(0, "early")
+        gather_s(0, 1, "early")
+        gather_s(1, 1, "early")
+        cast_w(0, "v")
+        gather_s(2, 1, "w_raw0")
+        quant_w(0, "early")
         cast_w(1, "s")
-        cast_w(0, "s")
-        quant_w(0)
-        make_qa(2, 0, "s")
-        make_qa(1, 0, "s")
-        make_qa(3, 0, "s")
-        gather_s(0)
-        quant_x(1)
-        gather_w(1, 1)
+        gather_s(3, 1, "early")
+        quant_w(1, "early")
         make_qa(0, 0, "s")
-        gather_w(0, 1)
-        quant_w(1)
-        make_qa(3, 1, "s")
-        quant_qa(3)
-        part(3, 1, 2, "v")
-        make_qa(1, 1, "s")
-        quant_qa(1)
-        part(1, 0, 1, "v")
+        make_qa(1, 0, "s")
         make_qa(0, 1, "s")
-        quant_qa(0)
-        part(3, 0, 1, "v")
-        make_qa(4, 1, "v")
+        make_qa(1, 1, "s")
+        gather_w(0, 0, 1, "early")
+        gather_w(0, 1, 1, "early")
+        quant_qa(0, "early")
+        quant_qa(1, "early")
+        make_qa(2, 0, "s")
         make_qa(2, 1, "s")
-        quant_qa(2)
-        part(2, 1, 2, "v")
-        part(2, 0, 1, "v")
+        make_qa(3, 0, "s")
+        make_qa(3, 1, "s")
+        gather_w(0, 2, 1, "early")
+        quant_qa(2, "early")
+        quant_qa(3, "early")
+        gather_w(1, 0, 1, "early")
+        gather_w(1, 1, 1, "early")
+        gather_w(1, 2, 1, "late")
+        block(0, 1, 0, 1, "v")
+        block(1, 2, 0, 1, "v")
+        cast_x(1, "v")
+        block(0, 2, 1, 2, "v")
+        quant_x(1, "late")
+        block(2, 3, 0, 2, "v")
+        gather_w(0, 3, 1, "late")
+        block(3, 4, 0, 2, "v")
+        gather_w(1, 3, 1, "late")
+        block(0, 2, 2, 3, "v")
+        make_qa(4, 0, "s")
+        make_qa(4, 1, "s")
+        block(2, 4, 2, 3, "v")
+        quant_qa(4, None)
+        make_qa(5, 0, "s")
         make_qa(5, 1, "s")
-        part(0, 0, 1, "v")
-        part(1, 1, 2, "v")
+        block(0, 2, 3, 4, "v")
+        quant_qa(5, None)
         cast_wv(0, "v")
-        gather_w(1, 3)
-        gather_w(1, 2)
-        make_qa(4, 0, "v")
-        quant_qa(4)
-        gather_s(2)
-        part(1, 2, 4, "v")
-        make_qa(5, 0, "v")
-        quant_qa(5)
-        part(0, 1, 2, "v")
-        part(0, 2, 4, "v")
-        part(3, 2, 4, "v")
-        part(2, 2, 4, "v")
+        cast_wv(1, "v")
+        block(2, 4, 3, 4, "v")
+        quant_wv(None)
+        block(4, 5, 0, 2, "v")
         make_qa(6, 0, "v")
-        part(4, 2, 4, "v")
-        quant_wv()
-        part(4, 0, 2, "v")
         make_qa(6, 1, "v")
-        make_qa(7, 1, "s")
-        quant_qa(6)
-        value(1, 3, "v")
-        make_qa(7, 0, "s")
-        quant_qa(7)
-        part(5, 0, 2, "v")
-        value(0, 1, "v")
+        quant_qa(6, None)
+        block(4, 5, 2, 4, "v")
         value(0, 0, "s")
+        value(0, 1, "v")
         store1(0, 0, 2)
-        value(1, 0, "v")
+        block(5, 6, 0, 2, "v")
+        make_qa(7, 0, "v")
+        make_qa(7, 1, "v")
+        quant_qa(7, None)
+        value(1, 0, "s")
         value(1, 1, "v")
         store1(1, 0, 2)
-        part(6, 0, 2, "v")
-        part(6, 2, 4, "v")
-        part(7, 0, 2, "v")
-        part(5, 2, 4, "v")
-        value(0, 2, "v")
-        value(1, 2, "s")
-        store1(1, 2, 4)
+        block(5, 6, 2, 4, "v")
+        value(0, 2, "s")
         value(0, 3, "v")
         store1(0, 2, 4)
-        part(7, 2, 4, "v")
+        block(6, 7, 0, 2, "v")
+        value(1, 2, "v")
+        value(1, 3, "v")
+        store1(1, 2, 4)
+        block(6, 7, 2, 4, "v")
+        block(7, 8, 0, 2, "v")
+        block(7, 8, 2, 3, "v")
+        block(7, 8, 3, 4, "v")

from contextlib import ExitStack

import concourse.mybir as mybir

K, R, M, T, N, J = 512, 1024, 1024, 4096, 256, 2048
FLOPS = 2 * K * R * M + 2 * R * M * J + 2 * R * N * J

F32 = mybir.dt.float32
BF16 = mybir.dt.bfloat16
I32 = mybir.dt.int32
U32 = mybir.dt.uint32
U16 = mybir.dt.uint16
U8 = mybir.dt.uint8
FP8X4 = mybir.dt.float8_e4m3fn_x4
TANH = mybir.ActivationFunctionType.Tanh
COPY = mybir.ActivationFunctionType.Copy
MULT = mybir.AluOpType.mult
ADD = mybir.AluOpType.add

P = 128
PACK = 4
PASSES = 2
JW = 512
SCALE_ROW = (0, 4)
X_PIECES = [(0, 512), (512, 1024)]


def tile_list_mlat_cap_kernel(tc, x, w, tab_words, tab_scales, wv, offs, out_0, out_1):
    nc = tc.nc
    with ExitStack() as ctx:
        keep = ctx.enter_context(tc.tile_pool(name="keep", bufs=1))
        psum = ctx.enter_context(tc.psum_pool(name="psum", bufs=8))
        early = ctx.enter_context(tc.tile_pool(name="early", bufs=15))
        late = ctx.enter_context(tc.tile_pool(name="late", bufs=22))

        def tile(shape, dtype, name, tag=None):
            if tag == "late":
                return late.tile(shape, dtype, name=name, tag=tag, align_bytes=64)
            if tag == "early":
                return early.tile(shape, dtype, name=name, tag=tag, align_bytes=64)
            return keep.tile(shape, dtype, name=name, tag=tag or name, align_bytes=64)

        offsets = keep.tile([P, J // 16], U16, name="offsets")
        w_raw = [tile([P, PACK, 512], F32, "w_raw%d" % a) for a in range(PASSES)]
        x_raw = [tile([P, PACK, hi - lo], F32, "x_raw%d" % lo) for lo, hi in X_PIECES]
        words = [tile([P, T], I32, "words%d" % a) for a in range(PASSES)]
        plane = tile([P, T // 4], I32, "plane")
        w_bf = [tile([P, 2048], BF16, "w_bf%d" % a) for a in range(PASSES)]
        x_bf = [tile([P, 4 * (hi - lo)], BF16, "x_bf%d" % lo) for lo, hi in X_PIECES]
        qa_bf = {}
        values = {}
        held = {}

        w_rows = w.rearrange("(p j) r -> p j r", j=PACK)
        x_rows = x.rearrange("(p j) m -> p j m", j=PACK)
        out_rows = out_0.rearrange("(mt p) j -> p mt j", p=P)
        scale_rows = tab_scales.bitcast(I32)

        zero = tile([P, 1], F32, "zero")
        bias = tile([P, 1], F32, "bias")
        nc.vector.memset(plane[:, : T // 8], 0)
        nc.gpsimd.memset(plane[:, T // 8 :], 0)
        nc.vector.memset(zero[:], 0.0)
        nc.scalar.activation(bias[:], zero[:], TANH)

        def load_offsets():
            nc.sync.dma_start(offsets[:], offs)

        def load_w(a):
            nc.sync.dma_start(out=w_raw[a][:], in_=w_rows[:, :, 512 * a : 512 * (a + 1)])

        def load_x(h):
            nc.sync.dma_start(out=x_raw[h][:], in_=x_rows[:, :, X_PIECES[h][0] : X_PIECES[h][1]])

        def load_words(a):
            nc.sync.dma_start(out=words[a][:], in_=tab_words[a].rearrange("p t i -> p (t i)").bitcast(I32))

        def load_wv():
            held["wv"] = tile([P, PASSES, PACK, N], F32, "wv_raw", "x_raw0")
            nc.sync.dma_start(
                out=held["wv"][:].rearrange("p a j n -> p a (j n)"),
                in_=wv.rearrange("(a p j) n -> p a (j n)", a=PASSES, j=PACK),
            )

        def load_scales(q):
            nc.sync.dma_start(out=plane[32 * q : 32 * q + 8, :], in_=scale_rows[:, 4 * q : 4 * q + 4, :])

        def quantize(src, width, name, tag):
            codes = tile([P, width // 4], U32, name + "_codes", tag)
            scales = tile([P, width // 4], U8, name + "_scales")
            nc.vector.quantize_mx(out=codes[:].bitcast(FP8X4), scales=scales[:], in_=src)
            return codes, scales

        def copy_on(engine, out, in_):
            if engine == "s":
                nc.scalar.copy(out, in_)
            elif engine == "v":
                nc.vector.tensor_copy(out, in_)
            else:
                nc.gpsimd.tensor_scalar(out, in_, 1.0, 0.0, MULT, ADD)

        wq = {}
        xq = {}
        qa = {}
        wvq = {}
        gw = {}
        gs = {}

        def cast_w(a, engine, m0=0, m1=P):
            copy_on(
                engine,
                w_bf[a][:].rearrange("p (t m j) -> p m t j", t=4, j=4)[:, m0:m1],
                w_raw[a][:].rearrange("p j (m t) -> p m t j", t=4)[:, m0:m1],
            )

        def quant_w(a, tag):
            wq[a] = quantize(w_bf[a][:], 2048, "w%d" % a, tag)

        def interleave(engine, dst, src):
            copy_on(
                engine,
                dst.rearrange("p (c i j) -> p c j i", i=4, j=4),
                src.rearrange("p j (c i) -> p c j i", i=4),
            )

        def cast_x(h, engine, c0=0, c1=None):
            c1 = c1 or X_PIECES[h][1] - X_PIECES[h][0]
            interleave(engine, x_bf[h][:, 4 * c0 : 4 * c1], x_raw[h][:, :, c0:c1])

        def quant_x(h, tag):
            xq[h] = quantize(x_bf[h][:], 4 * (X_PIECES[h][1] - X_PIECES[h][0]), "x%d" % h, tag)

        def cast_wv(a, engine):
            if "wv_bf" not in held:
                held["wv_bf"] = tile([P, PASSES, 4 * N], BF16, "wv_bf", "x_bf0")
            interleave(engine, held["wv_bf"][:, a, :], held["wv"][:, a, :, :])

        def quant_wv(tag):
            wvq[0] = quantize(held["wv_bf"][:].rearrange("p a c -> p (a c)"), 2048, "wv", tag)

        def gather(src, dtype, j, n, name, tag=None):
            got = tile([P, n * JW], dtype, name, tag)
            cols = slice(j * JW // 16, (j + n) * JW // 16)
            nc.vector.tensor_copy(got[:], src[:].bitcast(dtype).indirect(offsets[:, cols]))
            return [got[:, i * JW : (i + 1) * JW] for i in range(n)]

        def gather_s(j, n=1, tag=None):
            for i, got in enumerate(gather(plane, U8, j, n, "gs%d" % j, tag)):
                gs[j + i] = got

        def gather_w(a, j, n=1, tag=None):
            for i, got in enumerate(gather(words[a], U32, j, n, "gw%d%d" % (a, j), tag)):
                gw[a, j + i] = got

        def mm(out, lhs, lhs_cols, rhs, rhs_scale, start, stop):
            nc.tensor.matmul_mx(
                out=out,
                lhsT=lhs[0][:, lhs_cols].bitcast(FP8X4),
                lhsT_scale=lhs[1][:, lhs_cols],
                rhs=rhs.bitcast(FP8X4),
                rhs_scale=rhs_scale,
                start=start,
                stop=stop,
            )

        def make_qa(mt, a, engine):
            h = [i for i, (lo, hi) in enumerate(X_PIECES) if lo <= mt * P < hi][0]
            c0 = mt * P - X_PIECES[h][0]
            if mt not in qa_bf:
                qa_bf[mt] = tile([P, PASSES, P, PACK], BF16, "qa_bf%d" % mt, "qa_bf%d" % (mt % 4))
            bank = psum.tile([P, PACK, P], F32, name="bank")
            for t in range(PACK):
                mm(bank[:, t, :], wq[a], slice(t * P, (t + 1) * P),
                   xq[h][0][:, c0 : c0 + P], xq[h][1][:, c0 : c0 + P], True, True)
            copy_on(engine, qa_bf[mt][:, a, :, :], bank[:].rearrange("p t m -> p m t"))

        def quant_qa(mt, tag):
            qa[mt] = quantize(qa_bf[mt][:].rearrange("p a m t -> p (a m t)"), 1024, "qa%d" % mt, tag)

        def product(lhs, c0, stride, j):
            bank = psum.tile([P, JW], F32, name="bank")
            for a in range(PASSES):
                mm(bank[:], lhs, slice(a * stride + c0, a * stride + c0 + P),
                   gw[a, j], gs[j][SCALE_ROW[a] : P, :], a == 0, a == PASSES - 1)
            return bank

        def block(m0, m1, j0, j1, engine):
            capped = late.tile([P, m1 - m0, (j1 - j0) * JW], F32, name="capped%d%d" % (m0, j0), tag="late", align_bytes=64)
            for mt in range(m0, m1):
                for j in range(j0, j1):
                    bank = product(qa[mt], 0, P, j)
                    nc.scalar.activation(capped[:, mt - m0, (j - j0) * JW : (j - j0 + 1) * JW], bank[:], TANH, bias=bias[:], scale=0.00390625)
            if engine == "v":
                nc.vector.tensor_scalar(capped[:], capped[:], 8.0, None, MULT)
            elif engine == "s":
                nc.scalar.activation(capped[:], capped[:], COPY, scale=8.0)
            else:
                nc.gpsimd.tensor_scalar(capped[:], capped[:], 8.0, 0.0, MULT, ADD)
            nc.sync.dma_start(out=out_rows[:, m0:m1, j0 * JW : j1 * JW], in_=capped[:])

        def value(nt, j, engine):
            key = (nt, j // 2)
            if key not in values:
                tag = (("w_bf0", "w_raw1"), ("w_bf1", "x_raw%d" % X_PIECES[-1][0]))[nt][j // 2]
                values[key] = tile([P, 2 * JW], F32, "values%d%d" % key, tag)
            bank = product(wvq[0], nt * P, N, j)
            copy_on(engine, values[key][:, (j % 2) * JW : (j % 2 + 1) * JW], bank[:])

        def store1(nt, j0, j1):
            cols = slice(j0 * JW, j1 * JW)
            nc.sync.dma_start(out=out_1[nt * P : (nt + 1) * P, cols], in_=values[nt, j0 // 2][:])

        load_x(0)
        load_offsets()
        load_scales(0)
        load_scales(1)
        load_scales(2)
        load_scales(3)
        load_w(0)
        load_w(1)
        load_words(0)
        load_words(1)
        load_x(1)
        cast_x(0, "v")
        load_wv()
        quant_x(0, "early")
        gather_s(0, 1, "early")
        gather_s(1, 1, "early")
        cast_w(0, "v")
        gather_s(2, 1, "w_raw0")
        quant_w(0, "early")
        cast_w(1, "s")
        gather_s(3, 1, "early")
        quant_w(1, "early")
        make_qa(0, 0, "s")
        make_qa(1, 0, "s")
        make_qa(0, 1, "s")
        make_qa(1, 1, "s")
        gather_w(0, 0, 1, "early")
        gather_w(0, 1, 1, "early")
        quant_qa(0, "early")
        quant_qa(1, "early")
        make_qa(2, 0, "s")
        make_qa(2, 1, "s")
        make_qa(3, 0, "s")
        make_qa(3, 1, "s")
        gather_w(0, 2, 1, "early")
        quant_qa(2, "early")
        quant_qa(3, "early")
        gather_w(1, 0, 1, "early")
        gather_w(1, 1, 1, "early")
        gather_w(1, 2, 1, "late")
        block(0, 1, 0, 1, "v")
        block(1, 2, 0, 1, "v")
        cast_x(1, "v")
        block(0, 2, 1, 2, "v")
        quant_x(1, "late")
        block(2, 3, 0, 2, "v")
        gather_w(0, 3, 1, "late")
        block(3, 4, 0, 2, "v")
        gather_w(1, 3, 1, "late")
        block(0, 2, 2, 3, "v")
        make_qa(4, 0, "s")
        make_qa(4, 1, "s")
        block(2, 4, 2, 3, "v")
        quant_qa(4, None)
        make_qa(5, 0, "s")
        make_qa(5, 1, "s")
        block(0, 2, 3, 4, "v")
        quant_qa(5, None)
        cast_wv(0, "v")
        cast_wv(1, "v")
        block(2, 4, 3, 4, "v")
        quant_wv(None)
        block(4, 5, 0, 2, "v")
        make_qa(6, 0, "v")
        make_qa(6, 1, "v")
        quant_qa(6, None)
        block(4, 5, 2, 4, "v")
        value(0, 0, "s")
        value(0, 1, "v")
        store1(0, 0, 2)
        block(5, 6, 0, 2, "v")
        make_qa(7, 0, "v")
        make_qa(7, 1, "v")
        quant_qa(7, None)
        value(1, 0, "s")
        value(1, 1, "v")
        store1(1, 0, 2)
        block(5, 6, 2, 4, "v")
        value(0, 2, "s")
        value(0, 3, "v")
        store1(0, 2, 4)
        block(6, 7, 0, 2, "v")
        value(1, 2, "v")
        value(1, 3, "v")
        store1(1, 2, 4)
        block(6, 7, 2, 4, "v")
        block(7, 8, 0, 2, "v")
        block(7, 8, 2, 3, "v")
        block(7, 8, 3, 4, "v")
